import numpy as np
import ml_dtypes


def mxq(x, axis, fmt="e4m3"):
    dtype, down = {"e4m3": (ml_dtypes.float8_e4m3fn, 7), "e5m2": (ml_dtypes.float8_e5m2, 14)}[fmt]
    v = np.moveaxis(np.asarray(x, np.float32).astype(ml_dtypes.bfloat16).astype(np.float64), axis, -1)
    blocks = v.reshape(v.shape[:-1] + (-1, 32))
    amax = np.abs(blocks).max(-1, keepdims=True)
    byte = np.maximum(np.where(amax > 0, np.frexp(amax)[1] - 1 + 127, 0) - down, 1)
    scale = np.exp2(byte - 127.0)
    codes = (blocks / scale).astype(np.float32).astype(dtype).astype(np.float64)
    return np.moveaxis((codes * scale).reshape(v.shape), -1, axis)


WIDE = False


def mx_kscale(k):
    if not WIDE:
        return np.ones(k)
    levels = np.array([10, -10, 5, -5, 0])
    if k % 512:
        return np.exp2(np.random.permutation(np.resize(levels, k // 32))).repeat(32)
    a = np.empty((k // 512, 16))
    for p in range(k // 512):
        a[p, :8] = np.random.permutation(np.resize(levels, 8))
        for g in range(8):
            far = levels[np.abs(levels - a[p, g]) >= 10]
            a[p, g + 8] = far[np.random.randint(len(far))]
    return np.exp2(a.ravel()).repeat(32)


def f64(x):
    return np.asarray(x).astype(np.float64)


def striped(idx):
    return np.tile(idx.reshape(-1, 16).T, (8, 1)).astype(np.uint16)


def unstriped(offs):
    return offs[:16].T.reshape(-1).astype(np.int64)


E2M1 = np.array([0.0, 0.5, 1.0, 1.5, 2.0, 3.0, 4.0, 6.0, -0.0, -0.5, -1.0, -1.5, -2.0, -3.0, -4.0, -6.0])


def pack_weight(w, fmt):
    k, n = w.shape
    w = f64(np.asarray(w, np.float32).astype(ml_dtypes.bfloat16)).reshape(k // 32, 32, n)
    amax = np.abs(w).max(1)
    if fmt == "e4m3":
        byte = np.frexp(amax)[1] - 1 + 127 - 7
    else:
        mant, ex = np.frexp(amax / 6.0)
        byte = np.where(mant > 0.5, ex, ex - 1) + 127
    byte = np.clip(np.where(amax > 0, byte, 1), 1, 254)
    scaled = (w * np.exp2(127.0 - byte)[:, None, :]).reshape(k, n).astype(np.float32)
    by_word = np.ascontiguousarray(scaled.reshape(k // 512, 128, 4, n).transpose(0, 1, 3, 2))
    if fmt == "e4m3":
        words = by_word.astype(ml_dtypes.float8_e4m3fn).view(np.uint8)
    else:
        c = by_word.astype(ml_dtypes.float4_e2m1fn).view(np.uint8) & 0xF
        words = (c[..., 0::2] | (c[..., 1::2] << 4)).reshape(k // 512, 128, 2 * n)
    return np.ascontiguousarray(words), np.ascontiguousarray(byte.astype(np.uint8).reshape(k // 512, 16, n))


def unpack_weight(words, scales, fmt):
    g, _, n = scales.shape
    words = np.ascontiguousarray(words).reshape(g, 128, n, -1)
    if fmt == "e4m3":
        vals = words.view(ml_dtypes.float8_e4m3fn).astype(np.float64)
    else:
        nib = np.empty((g, 128, n, 4), np.uint8)
        nib[..., 0::2] = words & 0xF
        nib[..., 1::2] = words >> 4
        vals = E2M1[nib]
    vals = vals * np.repeat(np.exp2(scales.astype(np.float64) - 127.0), 8, axis=1)[..., None]
    return vals.transpose(0, 1, 3, 2).reshape(g * 512, n)


def pack_table(v):
    words, scales = pack_weight(v, "e4m3")
    return np.concatenate([words.reshape(words.shape[0], -1), scales.reshape(scales.shape[0], -1)], axis=1)


def unpack_table(tab):
    g, t = tab.shape[0], tab.shape[1] // 528
    return unpack_weight(tab[:, :512 * t].reshape(g, 128, t, 4), tab[:, 512 * t:].reshape(g, 16, t), "e4m3")


K, M, T, S = 1024, 1024, 4096, 1536


def setup_inputs():
    n = np.random.standard_normal
    s = mx_kscale(K)[:, None]
    p_w4 = pack_weight(n((K, M)) / np.sqrt(K) / s, "e2m1")
    return {
        "tab": pack_table(n((K, T)) * s),
        "w4_words": p_w4[0],
        "w4_scales": p_w4[1],
        "dw": (0.3 * n((K, M)) / np.sqrt(K) / s).astype(np.float32),
        "b": (0.3 * n(1024)).astype(np.float32),
        "offs": striped(np.random.permutation(T)[:S]),
    }


def reference(tab, w4_words, w4_scales, dw, b, offs):
    tab_ = unpack_table(tab)[:, unstriped(offs)]
    w4_ = unpack_weight(w4_words, w4_scales, "e2m1")
    dw_ = mxq(f64(dw), 0, "e4m3")
    y = tab_.T @ w4_ + tab_.T @ dw_
    return y + f64(b)[None, :]

from contextlib import ExitStack

import concourse.mybir as mybir
from concourse.masks import make_identity

K, M, T, S = 1024, 1024, 4096, 1536
FLOPS = 2 * 2 * K * M * S

P = 128
PASSES = K // 512
COLS = 512
HALVES = M // COLS
PIECE = 512
SLICES = S // PIECE
TILES = PIECE // P
QCOLS = 256

F32 = mybir.dt.float32
BF16 = mybir.dt.bfloat16
I32 = mybir.dt.int32
U32 = mybir.dt.uint32
U16 = mybir.dt.uint16
U8 = mybir.dt.uint8
FP8X4 = mybir.dt.float8_e4m3fn_x4
FP4X4 = mybir.dt.float4_e2m1fn_x4
ADD = mybir.AluOpType.add


def tile_list_tabd_tm_bias_kernel(tc, tab, w4_words, w4_scales, dw, b, offs, out):
    nc = tc.nc
    with ExitStack() as ctx:
        keep = ctx.enter_context(tc.tile_pool(name="keep", bufs=1))
        results = ctx.enter_context(tc.tile_pool(name="results", bufs=8))
        psum = ctx.enter_context(tc.psum_pool(name="psum", bufs=8))

        offsets = keep.tile([P, S // 16], U16, name="offsets")
        nc.sync.dma_start(offsets[:], offs)

        tab_words = [keep.tile([P, T], I32, name=f"tab_words{a}", align_bytes=64) for a in range(PASSES)]
        tab_scales = [keep.tile([P, T // 4], I32, name=f"tab_scales{a}", align_bytes=64) for a in range(PASSES)]
        w4_codes = keep.tile([P, PASSES, 2 * M], U8, name="w4_codes", align_bytes=64)
        w4_planes = keep.tile([P, PASSES, M // 4], I32, name="w4_planes", align_bytes=64)

        nc.vector.memset(tab_scales[0][:], 0)
        nc.gpsimd.memset(w4_planes[:], 0)
        nc.vector.memset(tab_scales[1][:], 0)

        def load_tab_scales(a):
            rows = tab[a, 512 * T : 528 * T].rearrange("(q t) -> q t", q=16)
            for q in range(4):
                nc.sync.dma_start(tab_scales[a][32 * q : 32 * q + 4, :], rows[4 * q : 4 * q + 4, :].bitcast(I32))

        def load_tab_words(a):
            words = tab[a, 0 : 512 * T].rearrange("(p t) -> p t", p=P).bitcast(I32)
            for c in range(0, T, T // 2):
                nc.sync.dma_start(tab_words[a][:, c : c + T // 2], words[:, c : c + T // 2])

        def load_w4(h):
            cols = slice(2 * COLS * h, 2 * COLS * (h + 1))
            nc.sync.dma_start(w4_codes[:, :, cols].bitcast(I32), w4_words[:, :, cols].rearrange("a p n -> p a n").bitcast(I32))

        def load_w4_scales():
            for q in range(4):
                nc.scalar.dma_start(
                    w4_planes[32 * q : 32 * q + 4, :, :],
                    w4_scales[:, 4 * q : 4 * q + 4, :].rearrange("a q n -> q a n").bitcast(I32),
                )

        dw_raw = {}

        def load_dw(a, h, step=COLS):
            raw = keep.tile([P, 4, COLS], F32, name=f"dw_raw{a}{h}", align_bytes=64)
            src = dw[512 * a : 512 * (a + 1), COLS * h : COLS * (h + 1)].rearrange("(p j) n -> p j n", j=4)
            for c in range(0, COLS, step):
                nc.sync.dma_start(raw[:, :, c : c + step], src[:, :, c : c + step])
            dw_raw[a, h] = raw

        load_tab_scales(0)
        load_tab_words(0)
        load_w4(0)
        load_w4_scales()
        load_dw(0, 0)
        load_tab_scales(1)
        load_tab_words(1)
        load_dw(1, 0, QCOLS)
        load_w4(1)
        load_dw(0, 1)
        load_dw(1, 1)

        ident = keep.tile([P, P], F32, name="ident")
        make_identity(nc, ident[:])
        b_rows = keep.tile([P, P], F32, name="b_rows")
        nc.gpsimd.memset(b_rows[:], 0.0)
        nc.scalar.dma_start(b_rows[0 : M // P, :], b.rearrange("(c n) -> c n", n=P))
        bank = psum.tile([P, COLS], F32, name="acc")
        nc.tensor.transpose(bank[:, 0:P], b_rows[:], ident[:])
        b_cols = keep.tile([P, M // P], F32, name="b_cols")
        nc.scalar.copy(b_cols[:], bank[:, 0 : M // P])
        bias = keep.tile([P, M], F32, name="bias")
        for h in range(HALVES):
            bank = psum.tile([P, COLS], F32, name="acc")
            for c in range(COLS // P):
                col = h * (COLS // P) + c
                nc.tensor.transpose(bank[:, c * P : (c + 1) * P], b_cols[:, col : col + 1].to_broadcast([P, P]), ident[:])
            nc.scalar.copy(bias[:, COLS * h : COLS * (h + 1)], bank[:])

        words = {}
        planes = {}

        def gather_words(s, a):
            words[s, a] = keep.tile([P, PIECE], U32, name=f"words{s}{a}", align_bytes=64)
            nc.vector.tensor_copy(
                words[s, a][:], tab_words[a][:].bitcast(U32).indirect(offsets[:, s * PIECE // 16 : (s + 1) * PIECE // 16])
            )

        def gather_planes(s, a):
            planes[s, a] = keep.tile([P, PIECE], U8, name=f"planes{s}{a}", align_bytes=64)
            nc.vector.tensor_copy(
                planes[s, a][:], tab_scales[a][:].bitcast(U8).indirect(offsets[:, s * PIECE // 16 : (s + 1) * PIECE // 16])
            )

        dw_codes = {}
        dw_planes = {}

        dw_grouped = {}

        def interleave_dw(a, h):
            grouped = keep.tile([P, COLS, 4], BF16, name=f"dw_grouped{a}{h}", align_bytes=64)
            for c in range(0, COLS, QCOLS):
                cols = slice(c, c + QCOLS)
                nc.scalar.copy(grouped[:, cols, :], dw_raw[a, h][:, :, cols].rearrange("p j n -> p n j"))
            dw_grouped[a, h] = grouped

        def quantize_dw(a, h):
            codes = keep.tile([P, COLS], U32, name=f"dw_codes{a}{h}", align_bytes=64)
            plane = keep.tile([P, COLS], U8, name=f"dw_planes{a}{h}", align_bytes=64)
            grouped = dw_grouped[a, h]
            for c in range(0, COLS, QCOLS):
                cols = slice(c, c + QCOLS)
                nc.vector.quantize_mx(
                    out=codes[:, cols].bitcast(FP8X4), scales=plane[:, cols], in_=grouped[:, cols, :].rearrange("p n j -> p (n j)")
                )
            dw_codes[a, h] = codes
            dw_planes[a, h] = plane

        accs = {}

        def multiply(s, t, h, kind, a, start=False, stop=False):
            if start:
                accs[s, t, h] = psum.tile([P, COLS], F32, name="acc")
            cols = slice(COLS * h, COLS * (h + 1))
            if kind == "w4":
                rhs = w4_codes[:, a, 2 * COLS * h : 2 * COLS * (h + 1)].bitcast(FP4X4)
                rhs_scale = w4_planes[:, a, :].bitcast(U8)[:, cols]
            else:
                rhs = dw_codes[a, h][:].bitcast(FP8X4)
                rhs_scale = dw_planes[a, h][:]
            rows = slice(P * t, P * (t + 1))
            nc.tensor.matmul_mx(
                out=accs[s, t, h][:],
                lhsT=words[s, a][:, rows].bitcast(FP8X4),
                lhsT_scale=planes[s, a][:, rows],
                rhs=rhs,
                rhs_scale=rhs_scale,
                start=start,
                stop=stop,
            )

        def finish(s, t, h):
            result = results.tile([P, COLS], F32, name="result")
            cols = slice(COLS * h, COLS * (h + 1))
            nc.vector.tensor_tensor(result[:], accs[s, t, h][:], bias[:, cols], ADD)
            row = PIECE * s + P * t
            nc.sync.dma_start(out[row : row + P, cols], result[:])

        def whole(s, t, h):
            multiply(s, t, h, "w4", 0, start=True)
            multiply(s, t, h, "w4", 1)
            multiply(s, t, h, "dw", 0)
            multiply(s, t, h, "dw", 1, stop=True)
            finish(s, t, h)

        first = (0, 1)
        for s in range(SLICES):
            gather_planes(s, 0)
        for s in first:
            gather_words(s, 0)
            for t in range(TILES):
                multiply(s, t, 0, "w4", 0, start=True)
        gather_words(2, 0)
        interleave_dw(0, 0)
        quantize_dw(0, 0)
        for s in first:
            for t in range(TILES):
                multiply(s, t, 0, "dw", 0)
        for s in range(SLICES):
            gather_planes(s, 1)
        for s in first:
            gather_words(s, 1)
            for t in range(TILES):
                multiply(s, t, 0, "w4", 1)
        gather_words(2, 1)
        interleave_dw(1, 0)
        quantize_dw(1, 0)
        interleave_dw(0, 1)
        interleave_dw(1, 1)
        for s in first:
            for t in range(TILES):
                multiply(s, t, 0, "dw", 1, stop=True)
                finish(s, t, 0)
            quantize_dw(s, 1)
        for t in range(TILES):
            whole(2, t, 0)
        for s in range(SLICES):
            for t in range(TILES):
                whole(s, t, 1)
